import numpy as np
import ml_dtypes


def mxq(x, axis, fmt="e4m3"):
    dtype, down = {"e4m3": (ml_dtypes.float8_e4m3fn, 7), "e5m2": (ml_dtypes.float8_e5m2, 14)}[fmt]
    v = np.moveaxis(np.asarray(x, np.float32).astype(ml_dtypes.bfloat16).astype(np.float64), axis, -1)
    blocks = v.reshape(v.shape[:-1] + (-1, 32))
    amax = np.abs(blocks).max(-1, keepdims=True)
    byte = np.maximum(np.where(amax > 0, np.frexp(amax)[1] - 1 + 127, 0) - down, 1)
    scale = np.exp2(byte - 127.0)
    codes = (blocks / scale).astype(np.float32).astype(dtype).astype(np.float64)
    return np.moveaxis((codes * scale).reshape(v.shape), -1, axis)


WIDE = False


def mx_kscale(k):
    if not WIDE:
        return np.ones(k)
    levels = np.array([10, -10, 5, -5, 0])
    if k % 512:
        return np.exp2(np.random.permutation(np.resize(levels, k // 32))).repeat(32)
    a = np.empty((k // 512, 16))
    for p in range(k // 512):
        a[p, :8] = np.random.permutation(np.resize(levels, 8))
        for g in range(8):
            far = levels[np.abs(levels - a[p, g]) >= 10]
            a[p, g + 8] = far[np.random.randint(len(far))]
    return np.exp2(a.ravel()).repeat(32)


BF16 = ml_dtypes.bfloat16


def bf(x):
    return np.asarray(x, np.float32).astype(BF16)


def f64(x):
    return np.asarray(x).astype(np.float64)


E2M1 = np.array([0.0, 0.5, 1.0, 1.5, 2.0, 3.0, 4.0, 6.0, -0.0, -0.5, -1.0, -1.5, -2.0, -3.0, -4.0, -6.0])


def pack_weight(w, fmt):
    k, n = w.shape
    w = f64(bf(w)).reshape(k // 32, 32, n)
    amax = np.abs(w).max(1)
    if fmt == "e4m3":
        byte = np.frexp(amax)[1] - 1 + 127 - 7
    else:
        mant, ex = np.frexp(amax / 6.0)
        byte = np.where(mant > 0.5, ex, ex - 1) + 127
    byte = np.clip(np.where(amax > 0, byte, 1), 1, 254)
    scaled = (w * np.exp2(127.0 - byte)[:, None, :]).reshape(k, n).astype(np.float32)
    by_word = np.ascontiguousarray(scaled.reshape(k // 512, 128, 4, n).transpose(0, 1, 3, 2))
    if fmt == "e4m3":
        words = by_word.astype(ml_dtypes.float8_e4m3fn).view(np.uint8)
    else:
        c = by_word.astype(ml_dtypes.float4_e2m1fn).view(np.uint8) & 0xF
        words = c[..., 0::2] | (c[..., 1::2] << 4)
    return np.ascontiguousarray(words), np.ascontiguousarray(byte.astype(np.uint8).reshape(k // 512, 16, n))


def unpack_weight(words, scales, fmt):
    g, p, n, _ = words.shape
    if fmt == "e4m3":
        vals = np.ascontiguousarray(words).view(ml_dtypes.float8_e4m3fn).astype(np.float64)
    else:
        nib = np.empty((g, p, n, 4), np.uint8)
        nib[..., 0::2] = words & 0xF
        nib[..., 1::2] = words >> 4
        vals = E2M1[nib]
    vals = vals * np.repeat(np.exp2(scales.astype(np.float64) - 127.0), 8, axis=1)[..., None]
    return vals.transpose(0, 1, 3, 2).reshape(g * 512, n)
def pack4(w):
    words, scales = pack_weight(w, "e2m1")
    return words.reshape(words.shape[0], 128, -1), scales


def unpack4(words, scales):
    return unpack_weight(words.reshape(words.shape[0], 128, -1, 2), scales, "e2m1")


def planes(Y):
    n, m = Y.shape
    b = f64(bf(Y)).reshape(n // 32, 32, m)
    amax = np.abs(b).max(1)
    byte = np.clip(np.where(amax > 0, np.frexp(amax)[1] - 1 + 127 - 7, 1), 1, 254)
    codes = (b * np.exp2(127.0 - byte)[:, None, :]).reshape(n, m).astype(np.float32).astype(ml_dtypes.float8_e4m3fn).view(np.uint8)
    words = codes.reshape(n // 512, 128, 4, m).transpose(0, 1, 3, 2)
    return np.ascontiguousarray(words), np.ascontiguousarray(byte.astype(np.uint8).reshape(n // 512, 16, m))


T, H8, H4, DH, D = 1024, 4, 12, 128, 2048
K8, K4 = H8 * DH, H4 * DH
KEPT_GAIN = 2.0
WIDTH_GAIN = 0.5


def setup_inputs():
    s8 = mx_kscale(K8)
    s4 = mx_kscale(K4)
    g = WIDTH_GAIN * np.exp(0.8 * np.random.randn(D))
    o8 = KEPT_GAIN * np.random.randn(H8, T, DH) * s8.reshape(H8, 1, DH)
    o4 = np.random.randn(H4, T, DH) * s4.reshape(H4, 1, DH)
    o = np.concatenate([o8, o4], axis=0)
    w8 = np.random.randn(K8, D) * g / np.sqrt(K8 + K4) / s8[:, None]
    w4 = np.random.randn(K4, D) * g / np.sqrt(K8 + K4) / s4[:, None]
    w4_words, w4_scales = pack4(w4)
    bias = 0.4 * np.random.randn(D) * g
    x = np.random.randn(T, D) * g
    return {"o": bf(o), "w8": bf(w8), "w4_words": w4_words, "w4_scales": w4_scales,
            "bias": bf(bias), "x": bf(x)}


def reference(o, w8, w4_words, w4_scales, bias, x):
    o = f64(o)
    A8 = mxq(o[:H8].transpose(1, 0, 2).reshape(T, K8), 1, "e4m3")
    A4 = mxq(o[H8:].transpose(1, 0, 2).reshape(T, K4), 1, "e4m3")
    W8 = mxq(f64(w8), 0, "e4m3")
    W4 = unpack4(w4_words, w4_scales)
    y = (A8 @ W8) + (A4 @ W4) + f64(bias) + f64(x)
    words, scales = planes(y.T)
    return y, words, scales

@@ -1,0 +1,269 @@
+from contextlib import ExitStack
+
+import concourse.mybir as mybir
+from concourse.masks import make_identity
+
+T, H8, H4, DH, D = 1024, 4, 12, 128, 2048
+FLOPS = 2 * T * (H8 + H4) * DH * D
+
+F32 = mybir.dt.float32
+BF16 = mybir.dt.bfloat16
+I32 = mybir.dt.int32
+U32 = mybir.dt.uint32
+U8 = mybir.dt.uint8
+FP8X4 = mybir.dt.float8_e4m3fn_x4
+FP4X4 = mybir.dt.float4_e2m1fn_x4
+ADD = mybir.AluOpType.add
+
+P = 128
+PASSES = 4
+W4_PASSES = 3
+CHUNK = 512
+CHUNKS = D // CHUNK
+TILES = T // P
+STEPS = CHUNKS * TILES
+X_TILES = 4
+W8_PIECES = 4
+BANKS = 4
+
+
+def tile_mixed_precision_attention_output_g5_kernel(tc, o, w8, w4_words, w4_scales, bias, x, out_0, out_1, out_2):
+    nc = tc.nc
+    with ExitStack() as ctx:
+        keep = ctx.enter_context(tc.tile_pool(name="keep", bufs=1))
+        flow = ctx.enter_context(tc.tile_pool(name="flow", bufs=2))
+        psum = ctx.enter_context(tc.psum_pool(name="psum", bufs=1))
+        ctx.enter_context(tc.manual_schedule())
+
+        identity = keep.tile([P, P], F32, name="identity")
+        make_identity(nc, identity[:])
+
+        w4_scales_first = keep.tile([P, W4_PASSES, CHUNK], U8, name="w4_scales_first", align_bytes=64)
+        w4_scales_rest = keep.tile([P, W4_PASSES, D - CHUNK], U8, name="w4_scales_rest", align_bytes=64)
+        nc.vector.memset(w4_scales_first[:].bitcast(I32), 0)
+        nc.vector.memset(w4_scales_rest[:].bitcast(I32), 0)
+
+        o_rows, x_rows, w8_rows, w4_codes = {}, {}, {}, {}
+
+        def load_o(i):
+            t = keep.tile([P, (H8 + H4) * DH], BF16, name="o_rows%d" % (i), align_bytes=64)
+            nc.sync.dma_start(out=t[:].rearrange("p (h d) -> p h d", d=DH), in_=o[:, i * P : (i + 1) * P, :].rearrange("h p d -> p h d"))
+            o_rows[i] = t
+
+        def load_x(c, half):
+            t = keep.tile([P, X_TILES, CHUNK], BF16, name="x_rows%d_%d" % (c, half))
+            rows = x[half * X_TILES * P : (half + 1) * X_TILES * P, c * CHUNK : (c + 1) * CHUNK]
+            nc.sync.dma_start(out=t[:], in_=rows.rearrange("(j p) n -> p j n", p=P))
+            x_rows[c, half] = t
+
+        def load_w8(c):
+            t = keep.tile([P, 4, CHUNK], BF16, name="w8_rows%d" % (c))
+            nc.sync.dma_start(out=t[:], in_=w8[:, c * CHUNK : (c + 1) * CHUNK].rearrange("(p t) n -> p t n", t=4))
+            w8_rows[c] = t
+
+        def load_w4(c):
+            t = keep.tile([P, W4_PASSES, 2 * CHUNK], U8, name="w4_codes%d" % (c), align_bytes=64)
+            words = w4_words[:, :, 2 * c * CHUNK : 2 * (c + 1) * CHUNK].rearrange("g p b -> p g b")
+            nc.sync.dma_start(out=t[:].bitcast(I32), in_=words.bitcast(I32))
+            w4_codes[c] = t
+
+        def load_w4_scales(plane, first, last):
+            for r in range(4):
+                rows = w4_scales[:, r:16:4, first:last].rearrange("g q n -> q g n")
+                nc.sync.dma_start(out=plane[r:P:32, :, :].bitcast(I32), in_=rows.bitcast(I32))
+
+        bias_rows = keep.tile([P, D // P], BF16, name="bias_rows")
+
+        load_o(0)
+        nc.sync.dma_start(out=bias_rows[:], in_=bias.rearrange("(p c) -> p c", p=P))
+        load_w8(0)
+        load_w4(0)
+        load_w4_scales(w4_scales_first, 0, CHUNK)
+        load_o(1)
+        load_x(0, 0)
+        load_o(2)
+        load_o(3)
+        load_w8(1)
+        load_o(4)
+        load_x(0, 1)
+        load_o(5)
+        load_o(6)
+        load_o(7)
+        load_w4(1)
+        load_w4_scales(w4_scales_rest, CHUNK, D)
+        for c in range(1, CHUNKS):
+            load_x(c, 0)
+            if c + 1 < CHUNKS:
+                load_w8(c + 1)
+            load_x(c, 1)
+            if c + 1 < CHUNKS:
+                load_w4(c + 1)
+
+        turned = []
+
+        def turn_bank():
+            t = psum.tile([P, 4, P], F32, name="turn%d" % (len(turned) % BANKS))
+            turned.append(t)
+            return t
+
+        a_codes, a_scales, a_grouped = {}, {}, {}
+        a_banks = {}
+
+        def turn_a(i):
+            words = o_rows[i][:].bitcast(F32)
+            banks = []
+            for b in range(2):
+                bank = turn_bank()
+                for s in range(4):
+                    c, u = 2 * b + s // 2, s % 2
+                    nc.tensor.transpose(bank[:, s, :], words[:, 256 * c + u : 256 * (c + 1) : 2], identity[:])
+                banks.append(bank)
+            a_banks[i] = banks
+
+        def copy_a(i):
+            g = flow.tile([P, PASSES * P * 4], BF16, name="a_grouped", bufs=3, align_bytes=64)
+            words = g[:].bitcast(F32).rearrange("p (c r u) -> p c r u", c=PASSES, u=2)
+            for b in range(2):
+                nc.scalar.copy(out=words[:, 2 * b : 2 * b + 2, :, :], in_=a_banks[i][b][:].rearrange("p (c u) r -> p c r u", u=2))
+            a_grouped[i] = g
+
+        def quantise_a(i):
+            codes = keep.tile([P, PASSES * P], U32, name="a_codes%d" % (i), align_bytes=64)
+            scales = keep.tile([P, PASSES * P], U8, name="a_scales%d" % (i), align_bytes=64)
+            nc.vector.quantize_mx(out=codes[:].bitcast(FP8X4), scales=scales[:], in_=a_grouped[i][:])
+            a_codes[i], a_scales[i] = codes, scales
+
+        bias_all = keep.tile([P, D], BF16, name="bias_all")
+
+        def spread_bias():
+            words = bias_rows[:].bitcast(F32)
+            spread = bias_all[:].bitcast(F32).rearrange("p (q w) -> p q w", w=8)
+            banks = []
+            for b in range(2):
+                bank = turn_bank()
+                for s in range(4):
+                    w = 4 * b + s
+                    nc.tensor.transpose(bank[:, s, :], words[:, w : w + 1].to_broadcast([P, P]), identity[:])
+                banks.append(bank)
+            for b in range(2):
+                nc.scalar.copy(out=spread[:, :, 4 * b : 4 * b + 4], in_=banks[b][:].rearrange("p w q -> p q w"))
+
+        w8_grouped, w8_codes, w8_scales = {}, {}, {}
+
+        def group_w8(c, copy, first, last):
+            if c not in w8_grouped:
+                g = flow.tile([P, CHUNK, 4], BF16, name="w8_grouped", bufs=2, align_bytes=64)
+                w8_grouped[c] = g
+            copy(out=w8_grouped[c][:, first:last, :].rearrange("p (n i) t -> p n t i", i=4),
+                 in_=w8_rows[c][:, :, first:last].rearrange("p t (n i) -> p n t i", i=4))
+
+        def quantise_w8(c):
+            codes = keep.tile([P, CHUNK], U32, name="w8_codes%d" % (c), align_bytes=64)
+            scales = keep.tile([P, CHUNK], U8, name="w8_scales%d" % (c), align_bytes=64)
+            nc.vector.quantize_mx(out=codes[:].bitcast(FP8X4), scales=scales[:], in_=w8_grouped[c][:].rearrange("p n t -> p (n t)"))
+            w8_codes[c], w8_scales[c] = codes, scales
+
+        addends, sums, y_pairs, y_sorted, y_banks, y_grouped = {}, {}, {}, {}, {}, {}
+        y_scales = keep.tile([P, T], U8, name="y_scales", align_bytes=64)
+
+        def add_bias(s):
+            c, i = divmod(s, TILES)
+            t = flow.tile([P, CHUNK], F32, name="addend", bufs=4)
+            nc.vector.tensor_tensor(out=t[:], in0=x_rows[c, i // X_TILES][:, i % X_TILES, :], in1=bias_all[:, c * CHUNK : (c + 1) * CHUNK], op=ADD)
+            addends[s] = t
+
+        def multiply(s):
+            c, i = divmod(s, TILES)
+            acc = psum.tile([P, CHUNK], F32, name="sum%d" % (s % BANKS))
+            for n, k in enumerate((1, 2, 3, 0)):
+                cols = slice(k * P, (k + 1) * P)
+                if k == 0:
+                    rhs, rhs_scale = w8_codes[c][:].bitcast(FP8X4), w8_scales[c][:]
+                elif c == 0:
+                    rhs, rhs_scale = w4_codes[c][:, k - 1, :].bitcast(FP4X4), w4_scales_first[:, k - 1, :]
+                else:
+                    rhs, rhs_scale = w4_codes[c][:, k - 1, :].bitcast(FP4X4), w4_scales_rest[:, k - 1, (c - 1) * CHUNK : c * CHUNK]
+                nc.tensor.matmul_mx(out=acc[:], lhsT=a_codes[i][:, cols].bitcast(FP8X4), lhsT_scale=a_scales[i][:, cols],
+                                    rhs=rhs, rhs_scale=rhs_scale, start=(n == 0), stop=(n == PASSES - 1))
+            sums[s] = acc
+
+        def finish_y(s):
+            c, i = divmod(s, TILES)
+            if s % 2 == 0:
+                t = flow.tile([P, 2, CHUNK], F32, name="y_pair", bufs=8)
+                y_pairs[s // 2] = t
+            y = y_pairs[s // 2]
+            nc.vector.tensor_tensor(out=y[:, s % 2, :], in0=sums[s][:], in1=addends[s][:], op=ADD)
+            if s % 2 == 1:
+                rows = out_0[(i - 1) * P : (i + 1) * P, c * CHUNK : (c + 1) * CHUNK]
+                nc.sync.dma_start(out=rows.rearrange("(j p) n -> p j n", p=P), in_=y[:])
+
+        def round_y(s):
+            t = flow.tile([P, CHUNK], BF16, name="y_sorted", bufs=5, align_bytes=64)
+            nc.scalar.copy(out=t[:].rearrange("p (u q e) -> p u q e", u=2, e=2),
+                           in_=y_pairs[s // 2][:, s % 2, :].rearrange("p (q u e) -> p u q e", u=2, e=2))
+            y_sorted[s] = t
+
+        def turn_y(pair):
+            bank = turn_bank()
+            for j in range(2):
+                words = y_sorted[2 * pair + j][:].bitcast(F32)
+                for u in range(2):
+                    nc.tensor.transpose(bank[:, 2 * j + u, :], words[:, u * P : (u + 1) * P], identity[:])
+            y_banks[pair] = bank
+
+        def copy_y(pair):
+            g = flow.tile([P, 2 * P * 4], BF16, name="y_grouped", bufs=3, align_bytes=64)
+            nc.scalar.copy(out=g[:].bitcast(F32).rearrange("p (j r u) -> p j r u", j=2, u=2),
+                           in_=y_banks[pair][:].rearrange("p (j u) r -> p j r u", u=2))
+            y_grouped[pair] = g
+
+        def quantise_y(pair):
+            c, k = divmod(pair, TILES // 2)
+            codes = flow.tile([P, 2 * P], U32, name="y_codes", bufs=8, align_bytes=64)
+            tokens = slice(2 * P * k, 2 * P * (k + 1))
+            nc.vector.quantize_mx(out=codes[:].bitcast(FP8X4), scales=y_scales[4 * c : P, tokens], in_=y_grouped[pair][:])
+            nc.sync.dma_start(out=out_1[c].rearrange("p m t -> p (m t)").bitcast(I32)[:, tokens], in_=codes[:].bitcast(I32))
+
+        turn_a(0)
+        copy_a(0)
+        group_w8(0, nc.vector.tensor_copy, 0, CHUNK)
+        quantise_a(0)
+        spread_bias()
+        turn_a(1)
+        copy_a(1)
+        quantise_w8(0)
+        quantise_a(1)
+        add_bias(0)
+        add_bias(1)
+
+        piece = CHUNK // W8_PIECES
+        for s in range(STEPS + 3):
+            c, i = divmod(s, TILES)
+            late_pair = (s - 2) // 2
+            if s < STEPS:
+                multiply(s)
+            if s + 2 < TILES:
+                turn_a(s + 2)
+            if s % 2 == 1 and s >= 3:
+                turn_y(late_pair)
+            if s + 2 < TILES:
+                copy_a(s + 2)
+            if s % 2 == 1 and s >= 3:
+                copy_y(late_pair)
+            if s < STEPS:
+                finish_y(s)
+                round_y(s)
+            if s % 2 == 0 and s >= 4:
+                quantise_y((s - 3) // 2)
+            if s + 2 < STEPS:
+                add_bias(s + 2)
+            if s + 2 < TILES:
+                quantise_a(s + 2)
+            if c + 1 < CHUNKS and 2 <= i < 2 + W8_PIECES:
+                group_w8(c + 1, nc.scalar.copy, (i - 2) * piece, (i - 1) * piece)
+            if c + 1 < CHUNKS and i == 2 + W8_PIECES:
+                quantise_w8(c + 1)
+
+        for q in range(4):
+            nc.sync.dma_start(out=out_2[:, 4 * q : 4 * q + 4, :].bitcast(I32), in_=y_scales[32 * q : 32 * q + 16, :].bitcast(I32))

@@ -25,6 +25,7 @@ STEPS = CHUNKS * TILES
 X_TILES = 4
 W8_PIECES = 4
 BANKS = 4
+LEAD = 4
 
 
 def tile_mixed_precision_attention_output_g5_kernel(tc, o, w8, w4_words, w4_scales, bias, x, out_0, out_1, out_2):
@@ -82,22 +83,21 @@ def tile_mixed_precision_attention_output_g5_kernel(tc, o, w8, w4_words, w4_scal
         load_o(1)
         load_x(0, 0)
         load_o(2)
-        load_o(3)
         load_w8(1)
-        load_o(4)
-        load_x(0, 1)
-        load_o(5)
-        load_o(6)
-        load_o(7)
+        load_o(3)
         load_w4(1)
         load_w4_scales(w4_scales_rest, CHUNK, D)
-        for c in range(1, CHUNKS):
+        load_x(1, 0)
+        for c in range(2, CHUNKS):
+            load_w8(c)
+            load_o(2 + c)
+            load_w4(c)
             load_x(c, 0)
-            if c + 1 < CHUNKS:
-                load_w8(c + 1)
-            load_x(c, 1)
-            if c + 1 < CHUNKS:
-                load_w4(c + 1)
+
+        def place(s):
+            half, rest = divmod(s, CHUNKS * X_TILES)
+            c, j = divmod(rest, X_TILES)
+            return c, half * X_TILES + j
 
         turned = []
 
@@ -167,13 +167,13 @@ def tile_mixed_precision_attention_output_g5_kernel(tc, o, w8, w4_words, w4_scal
         y_scales = keep.tile([P, T], U8, name="y_scales", align_bytes=64)
 
         def add_bias(s):
-            c, i = divmod(s, TILES)
-            t = flow.tile([P, CHUNK], F32, name="addend", bufs=4)
-            nc.vector.tensor_tensor(out=t[:], in0=x_rows[c, i // X_TILES][:, i % X_TILES, :], in1=bias_all[:, c * CHUNK : (c + 1) * CHUNK], op=ADD)
+            c, i = place(s)
+            t = flow.tile([P, CHUNK], F32, name="addend", bufs=LEAD + 1)
+            nc.gpsimd.tensor_tensor(out=t[:], in0=x_rows[c, i // X_TILES][:, i % X_TILES, :], in1=bias_all[:, c * CHUNK : (c + 1) * CHUNK], op=ADD)
             addends[s] = t
 
         def multiply(s):
-            c, i = divmod(s, TILES)
+            c, i = place(s)
             acc = psum.tile([P, CHUNK], F32, name="sum%d" % (s % BANKS))
             for n, k in enumerate((1, 2, 3, 0)):
                 cols = slice(k * P, (k + 1) * P)
@@ -187,43 +187,50 @@ def tile_mixed_precision_attention_output_g5_kernel(tc, o, w8, w4_words, w4_scal
                                     rhs=rhs, rhs_scale=rhs_scale, start=(n == 0), stop=(n == PASSES - 1))
             sums[s] = acc
 
+        def group_of(s):
+            return (s, s + 1) if s >= STEPS - 2 else (s - s % 2, s - s % 2 + 2)
+
         def finish_y(s):
-            c, i = divmod(s, TILES)
-            if s % 2 == 0:
+            first, last = group_of(s)
+            if s == first:
                 t = flow.tile([P, 2, CHUNK], F32, name="y_pair", bufs=8)
-                y_pairs[s // 2] = t
-            y = y_pairs[s // 2]
-            nc.vector.tensor_tensor(out=y[:, s % 2, :], in0=sums[s][:], in1=addends[s][:], op=ADD)
-            if s % 2 == 1:
-                rows = out_0[(i - 1) * P : (i + 1) * P, c * CHUNK : (c + 1) * CHUNK]
-                nc.sync.dma_start(out=rows.rearrange("(j p) n -> p j n", p=P), in_=y[:])
+                y_pairs[first] = t
+            y = y_pairs[first]
+            nc.vector.tensor_tensor(out=y[:, s - first, :], in0=sums[s][:], in1=addends[s][:], op=ADD)
+            if s == last - 1:
+                c, i = place(first)
+                rows = out_0[i * P : (i + last - first) * P, c * CHUNK : (c + 1) * CHUNK]
+                nc.sync.dma_start(out=rows.rearrange("(j p) n -> p j n", p=P), in_=y[:, : last - first, :])
 
         def round_y(s):
-            t = flow.tile([P, CHUNK], BF16, name="y_sorted", bufs=5, align_bytes=64)
+            first, last = group_of(s)
+            t = flow.tile([P, CHUNK], BF16, name="y_sorted", bufs=7, align_bytes=64)
             nc.scalar.copy(out=t[:].rearrange("p (u q e) -> p u q e", u=2, e=2),
-                           in_=y_pairs[s // 2][:, s % 2, :].rearrange("p (q u e) -> p u q e", u=2, e=2))
+                           in_=y_pairs[first][:, s - first, :].rearrange("p (q u e) -> p u q e", u=2, e=2))
             y_sorted[s] = t
 
-        def turn_y(pair):
+        def turn_y(first):
             bank = turn_bank()
-            for j in range(2):
-                words = y_sorted[2 * pair + j][:].bitcast(F32)
+            for s in range(*group_of(first)):
+                words = y_sorted[s][:].bitcast(F32)
                 for u in range(2):
-                    nc.tensor.transpose(bank[:, 2 * j + u, :], words[:, u * P : (u + 1) * P], identity[:])
-            y_banks[pair] = bank
+                    nc.tensor.transpose(bank[:, 2 * (s - first) + u, :], words[:, u * P : (u + 1) * P], identity[:])
+            y_banks[first] = bank
 
-        def copy_y(pair):
-            g = flow.tile([P, 2 * P * 4], BF16, name="y_grouped", bufs=3, align_bytes=64)
-            nc.scalar.copy(out=g[:].bitcast(F32).rearrange("p (j r u) -> p j r u", j=2, u=2),
-                           in_=y_banks[pair][:].rearrange("p (j u) r -> p j r u", u=2))
-            y_grouped[pair] = g
+        def copy_y(first):
+            n = group_of(first)[1] - first
+            g = flow.tile([P, 2 * P * 4], BF16, name="y_grouped", bufs=4, align_bytes=64)
+            nc.scalar.copy(out=g[:, : n * P * 4].bitcast(F32).rearrange("p (j r u) -> p j r u", j=n, u=2),
+                           in_=y_banks[first][:, : 2 * n, :].rearrange("p (j u) r -> p j r u", u=2))
+            y_grouped[first] = g
 
-        def quantise_y(pair):
-            c, k = divmod(pair, TILES // 2)
+        def quantise_y(first):
+            n = group_of(first)[1] - first
+            c, i = place(first)
             codes = flow.tile([P, 2 * P], U32, name="y_codes", bufs=8, align_bytes=64)
-            tokens = slice(2 * P * k, 2 * P * (k + 1))
-            nc.vector.quantize_mx(out=codes[:].bitcast(FP8X4), scales=y_scales[4 * c : P, tokens], in_=y_grouped[pair][:])
-            nc.sync.dma_start(out=out_1[c].rearrange("p m t -> p (m t)").bitcast(I32)[:, tokens], in_=codes[:].bitcast(I32))
+            tokens = slice(P * i, P * (i + n))
+            nc.vector.quantize_mx(out=codes[:, : n * P].bitcast(FP8X4), scales=y_scales[4 * c : P, tokens], in_=y_grouped[first][:, : n * P * 4])
+            nc.sync.dma_start(out=out_1[c].rearrange("p m t -> p (m t)").bitcast(I32)[:, tokens], in_=codes[:, : n * P].bitcast(I32))
 
         turn_a(0)
         copy_a(0)
@@ -234,36 +241,58 @@ def tile_mixed_precision_attention_output_g5_kernel(tc, o, w8, w4_words, w4_scal
         copy_a(1)
         quantise_w8(0)
         quantise_a(1)
-        add_bias(0)
-        add_bias(1)
+        for s in range(LEAD):
+            add_bias(s)
 
-        piece = CHUNK // W8_PIECES
-        for s in range(STEPS + 3):
-            c, i = divmod(s, TILES)
-            late_pair = (s - 2) // 2
+        def a_tile_after(s):
+            if s < 2:
+                return [s + 2]
+            if s % 4 == 1 and 4 <= 3 + s // 4 < TILES:
+                return [3 + s // 4]
+            return []
+
+        def y_groups_after(s):
+            if s >= STEPS - 3:
+                return {STEPS - 3: [STEPS - 6], STEPS - 1: [STEPS - 4, STEPS - 2], STEPS: [STEPS - 1]}.get(s, [])
+            if s % 4 == 3:
+                return [first for first in (s - 5, s - 3) if first >= 0]
+            return []
+
+        waiting = []
+        for s in range(STEPS + 4):
+            c, i = place(min(s, STEPS - 1))
             if s < STEPS:
                 multiply(s)
-            if s + 2 < TILES:
-                turn_a(s + 2)
-            if s % 2 == 1 and s >= 3:
-                turn_y(late_pair)
-            if s + 2 < TILES:
-                copy_a(s + 2)
-            if s % 2 == 1 and s >= 3:
-                copy_y(late_pair)
+            for k in a_tile_after(s):
+                turn_a(k)
+            for first in y_groups_after(s):
+                turn_y(first)
+            for k in a_tile_after(s):
+                copy_a(k)
             if s < STEPS:
                 finish_y(s)
                 round_y(s)
-            if s % 2 == 0 and s >= 4:
-                quantise_y((s - 3) // 2)
-            if s + 2 < STEPS:
-                add_bias(s + 2)
-            if s + 2 < TILES:
-                quantise_a(s + 2)
-            if c + 1 < CHUNKS and 2 <= i < 2 + W8_PIECES:
-                group_w8(c + 1, nc.scalar.copy, (i - 2) * piece, (i - 1) * piece)
-            if c + 1 < CHUNKS and i == 2 + W8_PIECES:
-                quantise_w8(c + 1)
+            for first in y_groups_after(s):
+                copy_y(first)
+            if waiting:
+                quantise_y(waiting[0])
+                waiting.remove(waiting[0])
+            waiting.extend(y_groups_after(s))
+            if s + LEAD < STEPS:
+                add_bias(s + LEAD)
+            for k in a_tile_after(s):
+                quantise_a(k)
+            if s < (CHUNKS - 1) * X_TILES:
+                if i == 0:
+                    group_w8(c + 1, nc.vector.tensor_copy, 0, CHUNK // 2)
+                if i == 1:
+                    group_w8(c + 1, nc.scalar.copy, CHUNK // 2, CHUNK)
+                if i == 2:
+                    quantise_w8(c + 1)
+            if s in (5, 9):
+                load_o(5 + s // 4)
+            if s % 4 == 1 and 1 <= s // 4 < 1 + CHUNKS:
+                load_x(s // 4 - 1, 1)
 
         for q in range(4):
             nc.sync.dma_start(out=out_2[:, 4 * q : 4 * q + 4, :].bitcast(I32), in_=y_scales[32 * q : 32 * q + 16, :].bitcast(I32))

@@ -25,7 +25,12 @@ STEPS = CHUNKS * TILES
 X_TILES = 4
 W8_PIECES = 4
 BANKS = 4
-LEAD = 4
+LEAD = 2
+A_STEPS = (0, 1, 9, 13, 19, 21)
+SORT_LEAD = 3
+W8_SPLIT = 256
+O_STEP = 9
+X_STEPS = (7, 15)
 
 
 def tile_mixed_precision_attention_output_g5_kernel(tc, o, w8, w4_words, w4_scales, bias, x, out_0, out_1, out_2):
@@ -46,16 +51,18 @@ def tile_mixed_precision_attention_output_g5_kernel(tc, o, w8, w4_words, w4_scal
 
         o_rows, x_rows, w8_rows, w4_codes = {}, {}, {}, {}
 
-        def load_o(i):
-            t = keep.tile([P, (H8 + H4) * DH], BF16, name="o_rows%d" % (i), align_bytes=64)
-            nc.sync.dma_start(out=t[:].rearrange("p (h d) -> p h d", d=DH), in_=o[:, i * P : (i + 1) * P, :].rearrange("h p d -> p h d"))
-            o_rows[i] = t
+        def load_o(pair, b):
+            t = flow.tile([P, 8 * 2 * DH], BF16, name="o_rows", bufs=8, align_bytes=64)
+            rows = o[8 * b : 8 * b + 8, pair * 2 * P : (pair + 1) * 2 * P, :].rearrange("h (p j) d -> p h (j d)", j=2)
+            nc.sync.dma_start(out=t[:].rearrange("p (h e) -> p h e", h=8), in_=rows)
+            o_rows[pair, b] = t
 
-        def load_x(c, half):
-            t = keep.tile([P, X_TILES, CHUNK], BF16, name="x_rows%d_%d" % (c, half))
-            rows = x[half * X_TILES * P : (half + 1) * X_TILES * P, c * CHUNK : (c + 1) * CHUNK]
-            nc.sync.dma_start(out=t[:], in_=rows.rearrange("(j p) n -> p j n", p=P))
-            x_rows[c, half] = t
+        def load_x(pair, first, last):
+            t = keep.tile([P, 2, (last - first) * CHUNK], BF16, name="x_rows%d_%d" % (pair, first))
+            rows = x[pair * 2 * P : (pair + 1) * 2 * P, first * CHUNK : last * CHUNK]
+            nc.sync.dma_start(out=t[:], in_=rows.rearrange("(p j) n -> p j n", j=2))
+            for c in range(first, last):
+                x_rows[pair, c] = t[:, :, (c - first) * CHUNK : (c - first + 1) * CHUNK]
 
         def load_w8(c):
             t = keep.tile([P, 4, CHUNK], BF16, name="w8_rows%d" % (c))
@@ -75,29 +82,34 @@ def tile_mixed_precision_attention_output_g5_kernel(tc, o, w8, w4_words, w4_scal
 
         bias_rows = keep.tile([P, D // P], BF16, name="bias_rows")
 
-        load_o(0)
         nc.sync.dma_start(out=bias_rows[:], in_=bias.rearrange("(p c) -> p c", p=P))
+        load_o(0, 1)
+        load_o(0, 0)
         load_w8(0)
         load_w4(0)
         load_w4_scales(w4_scales_first, 0, CHUNK)
-        load_o(1)
-        load_x(0, 0)
-        load_o(2)
+        load_o(1, 1)
+        load_o(1, 0)
+        load_x(0, 0, 1)
+        load_x(1, 0, 1)
         load_w8(1)
-        load_o(3)
         load_w4(1)
         load_w4_scales(w4_scales_rest, CHUNK, D)
-        load_x(1, 0)
-        for c in range(2, CHUNKS):
-            load_w8(c)
-            load_o(2 + c)
-            load_w4(c)
-            load_x(c, 0)
+        load_x(0, 1, 4)
+        load_x(1, 1, 4)
+        load_w8(2)
+        load_w4(2)
+        load_o(2, 1)
+        load_o(2, 0)
+        load_w8(3)
+        load_w4(3)
 
         def place(s):
-            half, rest = divmod(s, CHUNKS * X_TILES)
-            c, j = divmod(rest, X_TILES)
-            return c, half * X_TILES + j
+            if s < STEPS // 2:
+                return divmod(s, X_TILES)
+            pair, rest = divmod(s, 2 * CHUNKS)
+            c, j = divmod(rest, 2)
+            return c, 2 * pair + j
 
         turned = []
 
@@ -109,22 +121,27 @@ def tile_mixed_precision_attention_output_g5_kernel(tc, o, w8, w4_words, w4_scal
         a_codes, a_scales, a_grouped = {}, {}, {}
         a_banks = {}
 
+        o_sorted = {}
+
+        def sort_o(i, copy):
+            for b in (1, 0):
+                t = flow.tile([P, 4 * P], F32, name="o_sorted", bufs=6)
+                words = o_rows[i // 2, b][:].bitcast(F32).rearrange("p (h j w) -> p h j w", h=8, j=2)[:, :, i % 2, :]
+                copy(out=t[:].rearrange("p (c u h w) -> p c u h w", c=2, u=2, h=4), in_=words.rearrange("p (c h) (w u) -> p c u h w", c=2, u=2))
+                o_sorted[i, b] = t
+
         def turn_a(i):
-            words = o_rows[i][:].bitcast(F32)
-            banks = []
-            for b in range(2):
+            for b in (1, 0):
                 bank = turn_bank()
-                for s in range(4):
-                    c, u = 2 * b + s // 2, s % 2
-                    nc.tensor.transpose(bank[:, s, :], words[:, 256 * c + u : 256 * (c + 1) : 2], identity[:])
-                banks.append(bank)
-            a_banks[i] = banks
+                for n in range(4):
+                    nc.tensor.transpose(bank[:, n, :], o_sorted[i, b][:, n * P : (n + 1) * P], identity[:])
+                a_banks[i, b] = bank
 
         def copy_a(i):
             g = flow.tile([P, PASSES * P * 4], BF16, name="a_grouped", bufs=3, align_bytes=64)
             words = g[:].bitcast(F32).rearrange("p (c r u) -> p c r u", c=PASSES, u=2)
-            for b in range(2):
-                nc.scalar.copy(out=words[:, 2 * b : 2 * b + 2, :, :], in_=a_banks[i][b][:].rearrange("p (c u) r -> p c r u", u=2))
+            for b in (1, 0):
+                nc.scalar.copy(out=words[:, 2 * b : 2 * b + 2, :, :], in_=a_banks[i, b][:].rearrange("p (c u) r -> p c r u", u=2))
             a_grouped[i] = g
 
         def quantise_a(i):
@@ -169,13 +186,13 @@ def tile_mixed_precision_attention_output_g5_kernel(tc, o, w8, w4_words, w4_scal
         def add_bias(s):
             c, i = place(s)
             t = flow.tile([P, CHUNK], F32, name="addend", bufs=LEAD + 1)
-            nc.gpsimd.tensor_tensor(out=t[:], in0=x_rows[c, i // X_TILES][:, i % X_TILES, :], in1=bias_all[:, c * CHUNK : (c + 1) * CHUNK], op=ADD)
+            nc.vector.tensor_tensor(out=t[:], in0=x_rows[i // 2, c][:, i % 2, :], in1=bias_all[:, c * CHUNK : (c + 1) * CHUNK], op=ADD)
             addends[s] = t
 
         def multiply(s):
             c, i = place(s)
             acc = psum.tile([P, CHUNK], F32, name="sum%d" % (s % BANKS))
-            for n, k in enumerate((1, 2, 3, 0)):
+            for n, k in enumerate((2, 3, 1, 0)):
                 cols = slice(k * P, (k + 1) * P)
                 if k == 0:
                     rhs, rhs_scale = w8_codes[c][:].bitcast(FP8X4), w8_scales[c][:]
@@ -187,73 +204,69 @@ def tile_mixed_precision_attention_output_g5_kernel(tc, o, w8, w4_words, w4_scal
                                     rhs=rhs, rhs_scale=rhs_scale, start=(n == 0), stop=(n == PASSES - 1))
             sums[s] = acc
 
-        def group_of(s):
-            return (s, s + 1) if s >= STEPS - 2 else (s - s % 2, s - s % 2 + 2)
-
         def finish_y(s):
-            first, last = group_of(s)
-            if s == first:
+            c, i = place(s)
+            j = s % 2
+            if j == 0:
                 t = flow.tile([P, 2, CHUNK], F32, name="y_pair", bufs=8)
-                y_pairs[first] = t
-            y = y_pairs[first]
-            nc.vector.tensor_tensor(out=y[:, s - first, :], in0=sums[s][:], in1=addends[s][:], op=ADD)
-            if s == last - 1:
-                c, i = place(first)
-                rows = out_0[i * P : (i + last - first) * P, c * CHUNK : (c + 1) * CHUNK]
-                nc.sync.dma_start(out=rows.rearrange("(j p) n -> p j n", p=P), in_=y[:, : last - first, :])
+                y_pairs[s] = t
+            y = y_pairs[s - j]
+            nc.vector.tensor_tensor(out=y[:, j, :], in0=sums[s][:], in1=addends[s][:], op=ADD)
+            rows = out_0[(i - j) * P : (i - j + 2) * P, c * CHUNK : (c + 1) * CHUNK].rearrange("(p j) n -> p j n", j=2)
+            if s >= STEPS - 2:
+                nc.sync.dma_start(out=rows[:, j, :], in_=y[:, j, :])
+            elif j == 1:
+                nc.sync.dma_start(out=rows, in_=y[:])
 
         def round_y(s):
-            first, last = group_of(s)
             t = flow.tile([P, CHUNK], BF16, name="y_sorted", bufs=7, align_bytes=64)
-            nc.scalar.copy(out=t[:].rearrange("p (u q e) -> p u q e", u=2, e=2),
-                           in_=y_pairs[first][:, s - first, :].rearrange("p (q u e) -> p u q e", u=2, e=2))
+            copy = nc.vector.tensor_copy if s == STEPS - 1 else nc.scalar.copy
+            copy(out=t[:].rearrange("p (u q e) -> p u q e", u=2, e=2),
+                 in_=y_pairs[s - s % 2][:, s % 2, :].rearrange("p (q u e) -> p u q e", u=2, e=2))
             y_sorted[s] = t
 
         def turn_y(first):
             bank = turn_bank()
-            for s in range(*group_of(first)):
-                words = y_sorted[s][:].bitcast(F32)
-                for u in range(2):
-                    nc.tensor.transpose(bank[:, 2 * (s - first) + u, :], words[:, u * P : (u + 1) * P], identity[:])
+            for n in range(4):
+                words = y_sorted[first + n // 2][:].bitcast(F32)
+                nc.tensor.transpose(bank[:, n, :], words[:, n % 2 * P : (n % 2 + 1) * P], identity[:])
             y_banks[first] = bank
 
         def copy_y(first):
-            n = group_of(first)[1] - first
             g = flow.tile([P, 2 * P * 4], BF16, name="y_grouped", bufs=4, align_bytes=64)
-            nc.scalar.copy(out=g[:, : n * P * 4].bitcast(F32).rearrange("p (j r u) -> p j r u", j=n, u=2),
-                           in_=y_banks[first][:, : 2 * n, :].rearrange("p (j u) r -> p j r u", u=2))
+            nc.scalar.copy(out=g[:].bitcast(F32).rearrange("p (r j u) -> p r j u", j=2, u=2),
+                           in_=y_banks[first][:].rearrange("p (j u) r -> p r j u", u=2))
             y_grouped[first] = g
 
         def quantise_y(first):
-            n = group_of(first)[1] - first
             c, i = place(first)
             codes = flow.tile([P, 2 * P], U32, name="y_codes", bufs=8, align_bytes=64)
-            tokens = slice(P * i, P * (i + n))
-            nc.vector.quantize_mx(out=codes[:, : n * P].bitcast(FP8X4), scales=y_scales[4 * c : P, tokens], in_=y_grouped[first][:, : n * P * 4])
-            nc.sync.dma_start(out=out_1[c].rearrange("p m t -> p (m t)").bitcast(I32)[:, tokens], in_=codes[:, : n * P].bitcast(I32))
+            tokens = slice(P * i, P * (i + 2))
+            nc.vector.quantize_mx(out=codes[:].bitcast(FP8X4), scales=y_scales[4 * c : P, tokens], in_=y_grouped[first][:])
+            nc.sync.dma_start(out=out_1[c].rearrange("p m t -> p (m t)").bitcast(I32)[:, tokens], in_=codes[:].bitcast(I32))
 
+        spread_bias()
+        sort_o(0, nc.vector.tensor_copy)
         turn_a(0)
         copy_a(0)
+        sort_o(1, nc.vector.tensor_copy)
+        turn_a(1)
         group_w8(0, nc.vector.tensor_copy, 0, CHUNK)
         quantise_a(0)
-        spread_bias()
-        turn_a(1)
         copy_a(1)
         quantise_w8(0)
         quantise_a(1)
-        for s in range(LEAD):
-            add_bias(s)
+        sort_o(2, nc.vector.tensor_copy)
+        add_bias(0)
+        sort_o(3, nc.vector.tensor_copy)
+        add_bias(1)
 
         def a_tile_after(s):
-            if s < 2:
-                return [s + 2]
-            if s % 4 == 1 and 4 <= 3 + s // 4 < TILES:
-                return [3 + s // 4]
-            return []
+            return [2 + A_STEPS.index(s)] if s in A_STEPS else []
 
         def y_groups_after(s):
             if s >= STEPS - 3:
-                return {STEPS - 3: [STEPS - 6], STEPS - 1: [STEPS - 4, STEPS - 2], STEPS: [STEPS - 1]}.get(s, [])
+                return {STEPS - 3: [STEPS - 6], STEPS - 1: [STEPS - 4], STEPS: [STEPS - 2]}.get(s, [])
             if s % 4 == 3:
                 return [first for first in (s - 5, s - 3) if first >= 0]
             return []
@@ -267,32 +280,40 @@ def tile_mixed_precision_attention_output_g5_kernel(tc, o, w8, w4_words, w4_scal
                 turn_a(k)
             for first in y_groups_after(s):
                 turn_y(first)
-            for k in a_tile_after(s):
-                copy_a(k)
             if s < STEPS:
                 finish_y(s)
-                round_y(s)
+            for k in a_tile_after(s):
+                copy_a(k)
             for first in y_groups_after(s):
                 copy_y(first)
+            if s < STEPS:
+                round_y(s)
+            for k in a_tile_after(s if s < 2 else s - 1):
+                if (k < 4) == (s < 2):
+                    quantise_a(k)
             if waiting:
                 quantise_y(waiting[0])
                 waiting.remove(waiting[0])
             waiting.extend(y_groups_after(s))
             if s + LEAD < STEPS:
                 add_bias(s + LEAD)
-            for k in a_tile_after(s):
-                quantise_a(k)
+            for k in a_tile_after(s + SORT_LEAD):
+                if k >= 4:
+                    sort_o(k, nc.scalar.copy)
             if s < (CHUNKS - 1) * X_TILES:
+                if i == 0 and W8_SPLIT:
+                    group_w8(c + 1, nc.vector.tensor_copy, 0, W8_SPLIT)
                 if i == 0:
-                    group_w8(c + 1, nc.vector.tensor_copy, 0, CHUNK // 2)
+                    group_w8(c + 1, nc.scalar.copy, W8_SPLIT, (W8_SPLIT + CHUNK) // 2)
                 if i == 1:
-                    group_w8(c + 1, nc.scalar.copy, CHUNK // 2, CHUNK)
+                    group_w8(c + 1, nc.scalar.copy, (W8_SPLIT + CHUNK) // 2, CHUNK)
                 if i == 2:
                     quantise_w8(c + 1)
-            if s in (5, 9):
-                load_o(5 + s // 4)
-            if s % 4 == 1 and 1 <= s // 4 < 1 + CHUNKS:
-                load_x(s // 4 - 1, 1)
+            if s == O_STEP:
+                load_o(3, 1)
+                load_o(3, 0)
+            if s in X_STEPS:
+                load_x(2 + X_STEPS.index(s), 0, CHUNKS)
 
         for q in range(4):
-            nc.sync.dma_start(out=out_2[:, 4 * q : 4 * q + 4, :].bitcast(I32), in_=y_scales[32 * q : 32 * q + 16, :].bitcast(I32))
+            nc.scalar.dma_start(out=out_2[:, 4 * q : 4 * q + 4, :].bitcast(I32), in_=y_scales[32 * q : 32 * q + 16, :].bitcast(I32))

@@ -3,8 +3,8 @@ from contextlib import ExitStack
 import concourse.mybir as mybir
 from concourse.masks import make_identity
 
-T, H8, H4, DH, D = 1024, 4, 12, 128, 2048
-FLOPS = 2 * T * (H8 + H4) * DH * D
+T, HEADS, DH, D = 1024, 16, 128, 2048
+FLOPS = 2 * T * HEADS * DH * D
 
 F32 = mybir.dt.float32
 BF16 = mybir.dt.bfloat16
@@ -16,21 +16,47 @@ FP4X4 = mybir.dt.float4_e2m1fn_x4
 ADD = mybir.AluOpType.add
 
 P = 128
+PACK = 4
 PASSES = 4
 W4_PASSES = 3
 CHUNK = 512
 CHUNKS = D // CHUNK
 TILES = T // P
 STEPS = CHUNKS * TILES
-X_TILES = 4
-W8_PIECES = 4
+EARLY_TILES = 4
 BANKS = 4
-LEAD = 2
-A_STEPS = (0, 1, 9, 13, 19, 21)
+HALVES = (1, 0)
+PASS_ORDER = (2, 3, 1, 0)
+RUN = 4
+W8_SPLIT = 384
+ADDEND_LEAD = 2
+FIRST_LATE_TURN = 9
 SORT_LEAD = 3
-W8_SPLIT = 256
-O_STEP = 9
-X_STEPS = (7, 15)
+QUANTISE_LAG = 2
+LOAD_LEAD = 9
+
+
+def place(s):
+    if s < STEPS // 2:
+        return divmod(s, EARLY_TILES)
+    pair, rest = divmod(s, 2 * CHUNKS)
+    chunk, j = divmod(rest, 2)
+    return chunk, 2 * pair + j
+
+
+def late_tile_turned_after(s):
+    n, rest = divmod(s - FIRST_LATE_TURN, RUN)
+    return [EARLY_TILES + n] if rest == 0 and 0 <= n < TILES - EARLY_TILES else []
+
+
+def twins_turned_after(s):
+    if s == STEPS - 1:
+        return [STEPS - 6, STEPS - 4]
+    if s == STEPS:
+        return [STEPS - 2]
+    if s % RUN == 0 and s < STEPS:
+        return [twin for twin in (s - 6, s - 4) if twin >= 0]
+    return []
 
 
 def tile_mixed_precision_attention_output_g5_kernel(tc, o, w8, w4_words, w4_scales, bias, x, out_0, out_1, out_2):
@@ -51,104 +77,56 @@ def tile_mixed_precision_attention_output_g5_kernel(tc, o, w8, w4_words, w4_scal
 
         o_rows, x_rows, w8_rows, w4_codes = {}, {}, {}, {}
 
-        def load_o(pair, b):
-            t = flow.tile([P, 8 * 2 * DH], BF16, name="o_rows", bufs=8, align_bytes=64)
-            rows = o[8 * b : 8 * b + 8, pair * 2 * P : (pair + 1) * 2 * P, :].rearrange("h (p j) d -> p h (j d)", j=2)
-            nc.sync.dma_start(out=t[:].rearrange("p (h e) -> p h e", h=8), in_=rows)
-            o_rows[pair, b] = t
+        def load_o(pair):
+            for half in HALVES:
+                t = keep.tile([P, 8 * 2 * DH], BF16, name="o_rows%d_%d" % (pair, half), align_bytes=64)
+                rows = o[8 * half : 8 * half + 8, pair * 2 * P : (pair + 1) * 2 * P, :].rearrange("h (p j) d -> p h (j d)", j=2)
+                nc.sync.dma_start(out=t[:].rearrange("p (h e) -> p h e", h=8), in_=rows)
+                o_rows[pair, half] = t
 
         def load_x(pair, first, last):
             t = keep.tile([P, 2, (last - first) * CHUNK], BF16, name="x_rows%d_%d" % (pair, first))
             rows = x[pair * 2 * P : (pair + 1) * 2 * P, first * CHUNK : last * CHUNK]
             nc.sync.dma_start(out=t[:], in_=rows.rearrange("(p j) n -> p j n", j=2))
-            for c in range(first, last):
-                x_rows[pair, c] = t[:, :, (c - first) * CHUNK : (c - first + 1) * CHUNK]
+            for chunk in range(first, last):
+                x_rows[pair, chunk] = t[:, :, (chunk - first) * CHUNK : (chunk - first + 1) * CHUNK]
 
-        def load_w8(c):
-            t = keep.tile([P, 4, CHUNK], BF16, name="w8_rows%d" % (c))
-            nc.sync.dma_start(out=t[:], in_=w8[:, c * CHUNK : (c + 1) * CHUNK].rearrange("(p t) n -> p t n", t=4))
-            w8_rows[c] = t
+        def load_weights(chunk):
+            rows = keep.tile([P, PACK, CHUNK], BF16, name="w8_rows%d" % chunk)
+            nc.sync.dma_start(out=rows[:], in_=w8[:, chunk * CHUNK : (chunk + 1) * CHUNK].rearrange("(p t) n -> p t n", t=PACK))
+            w8_rows[chunk] = rows
+            codes = keep.tile([P, W4_PASSES, 2 * CHUNK], U8, name="w4_codes%d" % chunk, align_bytes=64)
+            source = w4_words[:, :, 2 * chunk * CHUNK : 2 * (chunk + 1) * CHUNK].rearrange("g p b -> p g b")
+            nc.sync.dma_start(out=codes[:].bitcast(I32), in_=source.bitcast(I32))
+            w4_codes[chunk] = codes
 
-        def load_w4(c):
-            t = keep.tile([P, W4_PASSES, 2 * CHUNK], U8, name="w4_codes%d" % (c), align_bytes=64)
-            words = w4_words[:, :, 2 * c * CHUNK : 2 * (c + 1) * CHUNK].rearrange("g p b -> p g b")
-            nc.sync.dma_start(out=t[:].bitcast(I32), in_=words.bitcast(I32))
-            w4_codes[c] = t
-
-        def load_w4_scales(plane, first, last):
+        def load_w4_scales(scales, first, last):
             for r in range(4):
                 rows = w4_scales[:, r:16:4, first:last].rearrange("g q n -> q g n")
-                nc.sync.dma_start(out=plane[r:P:32, :, :].bitcast(I32), in_=rows.bitcast(I32))
+                nc.sync.dma_start(out=scales[r:P:32, :, :].bitcast(I32), in_=rows.bitcast(I32))
 
         bias_rows = keep.tile([P, D // P], BF16, name="bias_rows")
-
         nc.sync.dma_start(out=bias_rows[:], in_=bias.rearrange("(p c) -> p c", p=P))
-        load_o(0, 1)
-        load_o(0, 0)
-        load_w8(0)
-        load_w4(0)
+        load_o(0)
+        load_weights(0)
         load_w4_scales(w4_scales_first, 0, CHUNK)
-        load_o(1, 1)
-        load_o(1, 0)
+        load_o(1)
         load_x(0, 0, 1)
         load_x(1, 0, 1)
-        load_w8(1)
-        load_w4(1)
+        load_weights(1)
         load_w4_scales(w4_scales_rest, CHUNK, D)
-        load_x(0, 1, 4)
-        load_x(1, 1, 4)
-        load_w8(2)
-        load_w4(2)
-        load_o(2, 1)
-        load_o(2, 0)
-        load_w8(3)
-        load_w4(3)
+        load_x(0, 1, CHUNKS)
+        load_x(1, 1, CHUNKS)
+        load_weights(2)
+        load_o(2)
+        load_weights(3)
 
-        def place(s):
-            if s < STEPS // 2:
-                return divmod(s, X_TILES)
-            pair, rest = divmod(s, 2 * CHUNKS)
-            c, j = divmod(rest, 2)
-            return c, 2 * pair + j
+        turn_banks = []
 
-        turned = []
-
-        def turn_bank():
-            t = psum.tile([P, 4, P], F32, name="turn%d" % (len(turned) % BANKS))
-            turned.append(t)
-            return t
-
-        a_codes, a_scales, a_grouped = {}, {}, {}
-        a_banks = {}
-
-        o_sorted = {}
-
-        def sort_o(i, copy):
-            for b in (1, 0):
-                t = flow.tile([P, 4 * P], F32, name="o_sorted", bufs=6)
-                words = o_rows[i // 2, b][:].bitcast(F32).rearrange("p (h j w) -> p h j w", h=8, j=2)[:, :, i % 2, :]
-                copy(out=t[:].rearrange("p (c u h w) -> p c u h w", c=2, u=2, h=4), in_=words.rearrange("p (c h) (w u) -> p c u h w", c=2, u=2))
-                o_sorted[i, b] = t
-
-        def turn_a(i):
-            for b in (1, 0):
-                bank = turn_bank()
-                for n in range(4):
-                    nc.tensor.transpose(bank[:, n, :], o_sorted[i, b][:, n * P : (n + 1) * P], identity[:])
-                a_banks[i, b] = bank
-
-        def copy_a(i):
-            g = flow.tile([P, PASSES * P * 4], BF16, name="a_grouped", bufs=3, align_bytes=64)
-            words = g[:].bitcast(F32).rearrange("p (c r u) -> p c r u", c=PASSES, u=2)
-            for b in (1, 0):
-                nc.scalar.copy(out=words[:, 2 * b : 2 * b + 2, :, :], in_=a_banks[i, b][:].rearrange("p (c u) r -> p c r u", u=2))
-            a_grouped[i] = g
-
-        def quantise_a(i):
-            codes = keep.tile([P, PASSES * P], U32, name="a_codes%d" % (i), align_bytes=64)
-            scales = keep.tile([P, PASSES * P], U8, name="a_scales%d" % (i), align_bytes=64)
-            nc.vector.quantize_mx(out=codes[:].bitcast(FP8X4), scales=scales[:], in_=a_grouped[i][:])
-            a_codes[i], a_scales[i] = codes, scales
+        def next_turn_bank():
+            bank = psum.tile([P, 4, P], F32, name="turn%d" % (len(turn_banks) % BANKS))
+            turn_banks.append(bank)
+            return bank
 
         bias_all = keep.tile([P, D], BF16, name="bias_all")
 
@@ -157,163 +135,175 @@ def tile_mixed_precision_attention_output_g5_kernel(tc, o, w8, w4_words, w4_scal
             spread = bias_all[:].bitcast(F32).rearrange("p (q w) -> p q w", w=8)
             banks = []
             for b in range(2):
-                bank = turn_bank()
-                for s in range(4):
-                    w = 4 * b + s
-                    nc.tensor.transpose(bank[:, s, :], words[:, w : w + 1].to_broadcast([P, P]), identity[:])
+                bank = next_turn_bank()
+                for n in range(4):
+                    w = 4 * b + n
+                    nc.tensor.transpose(bank[:, n, :], words[:, w : w + 1].to_broadcast([P, P]), identity[:])
                 banks.append(bank)
             for b in range(2):
                 nc.scalar.copy(out=spread[:, :, 4 * b : 4 * b + 4], in_=banks[b][:].rearrange("p w q -> p q w"))
 
+        o_sorted, a_banks, a_grouped, a_codes, a_scales = {}, {}, {}, {}, {}
+
+        def sort_o(tile, copy):
+            for half in HALVES:
+                t = flow.tile([P, 4 * P], F32, name="o_sorted", bufs=6)
+                words = o_rows[tile // 2, half][:].bitcast(F32).rearrange("p (h j w) -> p h j w", h=8, j=2)[:, :, tile % 2, :]
+                copy(out=t[:].rearrange("p (g u h w) -> p g u h w", g=2, u=2, h=4), in_=words.rearrange("p (g h) (w u) -> p g u h w", g=2, u=2))
+                o_sorted[tile, half] = t
+
+        def turn_o(tile):
+            for half in HALVES:
+                bank = next_turn_bank()
+                for n in range(4):
+                    nc.tensor.transpose(bank[:, n, :], o_sorted[tile, half][:, n * P : (n + 1) * P], identity[:])
+                a_banks[tile, half] = bank
+
+        def group_a(tile):
+            t = flow.tile([P, PASSES * P * PACK], BF16, name="a_grouped", bufs=3, align_bytes=64)
+            words = t[:].bitcast(F32).rearrange("p (g r u) -> p g r u", g=PASSES, u=2)
+            for half in HALVES:
+                nc.scalar.copy(out=words[:, 2 * half : 2 * half + 2, :, :], in_=a_banks[tile, half][:].rearrange("p (g u) r -> p g r u", u=2))
+            a_grouped[tile] = t
+
+        def quantise_a(tile):
+            codes = keep.tile([P, PASSES * P], U32, name="a_codes%d" % tile, align_bytes=64)
+            scales = keep.tile([P, PASSES * P], U8, name="a_scales%d" % tile, align_bytes=64)
+            nc.vector.quantize_mx(out=codes[:].bitcast(FP8X4), scales=scales[:], in_=a_grouped[tile][:])
+            a_codes[tile], a_scales[tile] = codes, scales
+
         w8_grouped, w8_codes, w8_scales = {}, {}, {}
 
-        def group_w8(c, copy, first, last):
-            if c not in w8_grouped:
-                g = flow.tile([P, CHUNK, 4], BF16, name="w8_grouped", bufs=2, align_bytes=64)
-                w8_grouped[c] = g
-            copy(out=w8_grouped[c][:, first:last, :].rearrange("p (n i) t -> p n t i", i=4),
-                 in_=w8_rows[c][:, :, first:last].rearrange("p t (n i) -> p n t i", i=4))
+        def group_w8(chunk):
+            t = flow.tile([P, CHUNK, PACK], BF16, name="w8_grouped", bufs=2, align_bytes=64)
+            for copy, first, last in ((nc.vector.tensor_copy, 0, W8_SPLIT), (nc.scalar.copy, W8_SPLIT, CHUNK)):
+                copy(out=t[:, first:last, :].rearrange("p (n i) t -> p n t i", i=4),
+                     in_=w8_rows[chunk][:, :, first:last].rearrange("p t (n i) -> p n t i", i=4))
+            w8_grouped[chunk] = t
 
-        def quantise_w8(c):
-            codes = keep.tile([P, CHUNK], U32, name="w8_codes%d" % (c), align_bytes=64)
-            scales = keep.tile([P, CHUNK], U8, name="w8_scales%d" % (c), align_bytes=64)
-            nc.vector.quantize_mx(out=codes[:].bitcast(FP8X4), scales=scales[:], in_=w8_grouped[c][:].rearrange("p n t -> p (n t)"))
-            w8_codes[c], w8_scales[c] = codes, scales
+        def quantise_w8(chunk):
+            codes = keep.tile([P, CHUNK], U32, name="w8_codes%d" % chunk, align_bytes=64)
+            scales = keep.tile([P, CHUNK], U8, name="w8_scales%d" % chunk, align_bytes=64)
+            nc.vector.quantize_mx(out=codes[:].bitcast(FP8X4), scales=scales[:], in_=w8_grouped[chunk][:].rearrange("p n t -> p (n t)"))
+            w8_codes[chunk], w8_scales[chunk] = codes, scales
 
-        addends, sums, y_pairs, y_sorted, y_banks, y_grouped = {}, {}, {}, {}, {}, {}
-        y_scales = keep.tile([P, T], U8, name="y_scales", align_bytes=64)
+        addends, products, y_twins = {}, {}, {}
 
         def add_bias(s):
-            c, i = place(s)
-            t = flow.tile([P, CHUNK], F32, name="addend", bufs=LEAD + 1)
-            nc.vector.tensor_tensor(out=t[:], in0=x_rows[i // 2, c][:, i % 2, :], in1=bias_all[:, c * CHUNK : (c + 1) * CHUNK], op=ADD)
+            chunk, tile = place(s)
+            t = flow.tile([P, CHUNK], F32, name="addend", bufs=ADDEND_LEAD + 1)
+            nc.vector.tensor_tensor(out=t[:], in0=x_rows[tile // 2, chunk][:, tile % 2, :], in1=bias_all[:, chunk * CHUNK : (chunk + 1) * CHUNK], op=ADD)
             addends[s] = t
 
         def multiply(s):
-            c, i = place(s)
-            acc = psum.tile([P, CHUNK], F32, name="sum%d" % (s % BANKS))
-            for n, k in enumerate((2, 3, 1, 0)):
-                cols = slice(k * P, (k + 1) * P)
-                if k == 0:
-                    rhs, rhs_scale = w8_codes[c][:].bitcast(FP8X4), w8_scales[c][:]
-                elif c == 0:
-                    rhs, rhs_scale = w4_codes[c][:, k - 1, :].bitcast(FP4X4), w4_scales_first[:, k - 1, :]
+            chunk, tile = place(s)
+            bank = psum.tile([P, CHUNK], F32, name="product%d" % (s % BANKS))
+            for g in PASS_ORDER:
+                if g == 0:
+                    rhs, rhs_scale = w8_codes[chunk][:].bitcast(FP8X4), w8_scales[chunk][:]
+                elif chunk == 0:
+                    rhs, rhs_scale = w4_codes[chunk][:, g - 1, :].bitcast(FP4X4), w4_scales_first[:, g - 1, :]
                 else:
-                    rhs, rhs_scale = w4_codes[c][:, k - 1, :].bitcast(FP4X4), w4_scales_rest[:, k - 1, (c - 1) * CHUNK : c * CHUNK]
-                nc.tensor.matmul_mx(out=acc[:], lhsT=a_codes[i][:, cols].bitcast(FP8X4), lhsT_scale=a_scales[i][:, cols],
-                                    rhs=rhs, rhs_scale=rhs_scale, start=(n == 0), stop=(n == PASSES - 1))
-            sums[s] = acc
+                    rhs, rhs_scale = w4_codes[chunk][:, g - 1, :].bitcast(FP4X4), w4_scales_rest[:, g - 1, (chunk - 1) * CHUNK : chunk * CHUNK]
+                tokens = slice(g * P, (g + 1) * P)
+                nc.tensor.matmul_mx(out=bank[:], lhsT=a_codes[tile][:, tokens].bitcast(FP8X4), lhsT_scale=a_scales[tile][:, tokens],
+                                    rhs=rhs, rhs_scale=rhs_scale, start=(g == PASS_ORDER[0]), stop=(g == PASS_ORDER[-1]))
+            products[s] = bank
 
         def finish_y(s):
-            c, i = place(s)
+            chunk, tile = place(s)
             j = s % 2
             if j == 0:
-                t = flow.tile([P, 2, CHUNK], F32, name="y_pair", bufs=8)
-                y_pairs[s] = t
-            y = y_pairs[s - j]
-            nc.vector.tensor_tensor(out=y[:, j, :], in0=sums[s][:], in1=addends[s][:], op=ADD)
-            rows = out_0[(i - j) * P : (i - j + 2) * P, c * CHUNK : (c + 1) * CHUNK].rearrange("(p j) n -> p j n", j=2)
+                t = flow.tile([P, 2, CHUNK], F32, name="y_twin", bufs=8)
+                y_twins[s] = t
+            y = y_twins[s - j]
+            nc.vector.tensor_tensor(out=y[:, j, :], in0=products[s][:], in1=addends[s][:], op=ADD)
+            rows = out_0[(tile - j) * P : (tile - j + 2) * P, chunk * CHUNK : (chunk + 1) * CHUNK].rearrange("(p j) n -> p j n", j=2)
             if s >= STEPS - 2:
                 nc.sync.dma_start(out=rows[:, j, :], in_=y[:, j, :])
             elif j == 1:
                 nc.sync.dma_start(out=rows, in_=y[:])
 
+        y_sorted, y_banks, y_grouped = {}, {}, {}
+        y_scales = keep.tile([P, T], U8, name="y_scales", align_bytes=64)
+
         def round_y(s):
-            t = flow.tile([P, CHUNK], BF16, name="y_sorted", bufs=7, align_bytes=64)
+            t = flow.tile([P, CHUNK], BF16, name="y_sorted", bufs=8, align_bytes=64)
             copy = nc.vector.tensor_copy if s == STEPS - 1 else nc.scalar.copy
             copy(out=t[:].rearrange("p (u q e) -> p u q e", u=2, e=2),
-                 in_=y_pairs[s - s % 2][:, s % 2, :].rearrange("p (q u e) -> p u q e", u=2, e=2))
+                 in_=y_twins[s - s % 2][:, s % 2, :].rearrange("p (q u e) -> p u q e", u=2, e=2))
             y_sorted[s] = t
 
-        def turn_y(first):
-            bank = turn_bank()
+        def turn_y(twin):
+            bank = next_turn_bank()
             for n in range(4):
-                words = y_sorted[first + n // 2][:].bitcast(F32)
-                nc.tensor.transpose(bank[:, n, :], words[:, n % 2 * P : (n % 2 + 1) * P], identity[:])
-            y_banks[first] = bank
+                j, u = divmod(n, 2)
+                nc.tensor.transpose(bank[:, n, :], y_sorted[twin + j][:].bitcast(F32)[:, u * P : (u + 1) * P], identity[:])
+            y_banks[twin] = bank
 
-        def copy_y(first):
-            g = flow.tile([P, 2 * P * 4], BF16, name="y_grouped", bufs=4, align_bytes=64)
-            nc.scalar.copy(out=g[:].bitcast(F32).rearrange("p (r j u) -> p r j u", j=2, u=2),
-                           in_=y_banks[first][:].rearrange("p (j u) r -> p r j u", u=2))
-            y_grouped[first] = g
+        def group_y(twin):
+            t = flow.tile([P, 2 * P * PACK], BF16, name="y_grouped", bufs=4, align_bytes=64)
+            nc.scalar.copy(out=t[:].bitcast(F32).rearrange("p (r j u) -> p r j u", j=2, u=2),
+                           in_=y_banks[twin][:].rearrange("p (j u) r -> p r j u", u=2))
+            y_grouped[twin] = t
 
-        def quantise_y(first):
-            c, i = place(first)
+        def quantise_y(twin):
+            chunk, tile = place(twin)
             codes = flow.tile([P, 2 * P], U32, name="y_codes", bufs=8, align_bytes=64)
-            tokens = slice(P * i, P * (i + 2))
-            nc.vector.quantize_mx(out=codes[:].bitcast(FP8X4), scales=y_scales[4 * c : P, tokens], in_=y_grouped[first][:])
-            nc.sync.dma_start(out=out_1[c].rearrange("p m t -> p (m t)").bitcast(I32)[:, tokens], in_=codes[:].bitcast(I32))
+            tokens = slice(P * tile, P * (tile + 2))
+            nc.vector.quantize_mx(out=codes[:].bitcast(FP8X4), scales=y_scales[4 * chunk : P, tokens], in_=y_grouped[twin][:])
+            nc.sync.dma_start(out=out_1[chunk].rearrange("p m t -> p (m t)").bitcast(I32)[:, tokens], in_=codes[:].bitcast(I32))
 
         spread_bias()
         sort_o(0, nc.vector.tensor_copy)
-        turn_a(0)
-        copy_a(0)
+        turn_o(0)
+        group_a(0)
         sort_o(1, nc.vector.tensor_copy)
-        turn_a(1)
-        group_w8(0, nc.vector.tensor_copy, 0, CHUNK)
+        turn_o(1)
+        group_w8(0)
         quantise_a(0)
-        copy_a(1)
+        group_a(1)
         quantise_w8(0)
         quantise_a(1)
         sort_o(2, nc.vector.tensor_copy)
         add_bias(0)
-        sort_o(3, nc.vector.tensor_copy)
+        sort_o(3, nc.scalar.copy)
         add_bias(1)
 
-        def a_tile_after(s):
-            return [2 + A_STEPS.index(s)] if s in A_STEPS else []
-
-        def y_groups_after(s):
-            if s >= STEPS - 3:
-                return {STEPS - 3: [STEPS - 6], STEPS - 1: [STEPS - 4], STEPS: [STEPS - 2]}.get(s, [])
-            if s % 4 == 3:
-                return [first for first in (s - 5, s - 3) if first >= 0]
-            return []
-
-        waiting = []
-        for s in range(STEPS + 4):
-            c, i = place(min(s, STEPS - 1))
+        for s in range(STEPS + 2):
+            early = [s + 2] if s + 2 < EARLY_TILES else []
             if s < STEPS:
                 multiply(s)
-            for k in a_tile_after(s):
-                turn_a(k)
-            for first in y_groups_after(s):
-                turn_y(first)
+            for tile in early + late_tile_turned_after(s):
+                turn_o(tile)
+            for twin in twins_turned_after(s):
+                turn_y(twin)
             if s < STEPS:
                 finish_y(s)
-            for k in a_tile_after(s):
-                copy_a(k)
-            for first in y_groups_after(s):
-                copy_y(first)
+            for tile in early + late_tile_turned_after(s):
+                group_a(tile)
+            for twin in twins_turned_after(s):
+                group_y(twin)
             if s < STEPS:
                 round_y(s)
-            for k in a_tile_after(s if s < 2 else s - 1):
-                if (k < 4) == (s < 2):
-                    quantise_a(k)
-            if waiting:
-                quantise_y(waiting[0])
-                waiting.remove(waiting[0])
-            waiting.extend(y_groups_after(s))
-            if s + LEAD < STEPS:
-                add_bias(s + LEAD)
-            for k in a_tile_after(s + SORT_LEAD):
-                if k >= 4:
-                    sort_o(k, nc.scalar.copy)
-            if s < (CHUNKS - 1) * X_TILES:
-                if i == 0 and W8_SPLIT:
-                    group_w8(c + 1, nc.vector.tensor_copy, 0, W8_SPLIT)
-                if i == 0:
-                    group_w8(c + 1, nc.scalar.copy, W8_SPLIT, (W8_SPLIT + CHUNK) // 2)
-                if i == 1:
-                    group_w8(c + 1, nc.scalar.copy, (W8_SPLIT + CHUNK) // 2, CHUNK)
-                if i == 2:
-                    quantise_w8(c + 1)
-            if s == O_STEP:
-                load_o(3, 1)
-                load_o(3, 0)
-            if s in X_STEPS:
-                load_x(2 + X_STEPS.index(s), 0, CHUNKS)
+            for tile in early + late_tile_turned_after(s - QUANTISE_LAG):
+                quantise_a(tile)
+            for twin in twins_turned_after(s - 1):
+                quantise_y(twin)
+            if s + ADDEND_LEAD < STEPS:
+                add_bias(s + ADDEND_LEAD)
+            for tile in late_tile_turned_after(s + SORT_LEAD):
+                sort_o(tile, nc.scalar.copy)
+            if s < (CHUNKS - 1) * EARLY_TILES:
+                if s % EARLY_TILES == 0:
+                    group_w8(s // EARLY_TILES + 1)
+                if s % EARLY_TILES == 2:
+                    quantise_w8(s // EARLY_TILES + 1)
+            if late_tile_turned_after(s + LOAD_LEAD + SORT_LEAD) == [TILES - 2]:
+                load_o(TILES // 2 - 1)
+            for pair in range(EARLY_TILES // 2, TILES // 2):
+                if s + LOAD_LEAD + ADDEND_LEAD == pair * 2 * CHUNKS:
+                    load_x(pair, 0, CHUNKS)
 
         for q in range(4):
             nc.scalar.dma_start(out=out_2[:, 4 * q : 4 * q + 4, :].bitcast(I32), in_=y_scales[32 * q : 32 * q + 16, :].bitcast(I32))

from contextlib import ExitStack

import concourse.mybir as mybir
from concourse.masks import make_identity

T, HEADS, DH, D = 1024, 16, 128, 2048
FLOPS = 2 * T * HEADS * DH * D

F32 = mybir.dt.float32
BF16 = mybir.dt.bfloat16
I32 = mybir.dt.int32
U32 = mybir.dt.uint32
U8 = mybir.dt.uint8
FP8X4 = mybir.dt.float8_e4m3fn_x4
FP4X4 = mybir.dt.float4_e2m1fn_x4
ADD = mybir.AluOpType.add

P = 128
PACK = 4
PASSES = 4
W4_PASSES = 3
CHUNK = 512
CHUNKS = D // CHUNK
TILES = T // P
STEPS = CHUNKS * TILES
EARLY_TILES = 4
BANKS = 4
HALVES = (1, 0)
PASS_ORDER = (2, 3, 1, 0)
RUN = 4
W8_SPLIT = 384
ADDEND_LEAD = 2
FIRST_LATE_TURN = 9
SORT_LEAD = 3
QUANTISE_LAG = 2
LOAD_LEAD = 9


def place(s):
    if s < STEPS // 2:
        return divmod(s, EARLY_TILES)
    pair, rest = divmod(s, 2 * CHUNKS)
    chunk, j = divmod(rest, 2)
    return chunk, 2 * pair + j


def late_tile_turned_after(s):
    n, rest = divmod(s - FIRST_LATE_TURN, RUN)
    return [EARLY_TILES + n] if rest == 0 and 0 <= n < TILES - EARLY_TILES else []


def twins_turned_after(s):
    if s == STEPS - 1:
        return [STEPS - 6, STEPS - 4]
    if s == STEPS:
        return [STEPS - 2]
    if s % RUN == 0 and s < STEPS:
        return [twin for twin in (s - 6, s - 4) if twin >= 0]
    return []


def tile_mixed_precision_attention_output_g5_kernel(tc, o, w8, w4_words, w4_scales, bias, x, out_0, out_1, out_2):
    nc = tc.nc
    with ExitStack() as ctx:
        keep = ctx.enter_context(tc.tile_pool(name="keep", bufs=1))
        flow = ctx.enter_context(tc.tile_pool(name="flow", bufs=2))
        psum = ctx.enter_context(tc.psum_pool(name="psum", bufs=1))
        ctx.enter_context(tc.manual_schedule())

        identity = keep.tile([P, P], F32, name="identity")
        make_identity(nc, identity[:])

        w4_scales_first = keep.tile([P, W4_PASSES, CHUNK], U8, name="w4_scales_first", align_bytes=64)
        w4_scales_rest = keep.tile([P, W4_PASSES, D - CHUNK], U8, name="w4_scales_rest", align_bytes=64)
        nc.vector.memset(w4_scales_first[:].bitcast(I32), 0)
        nc.vector.memset(w4_scales_rest[:].bitcast(I32), 0)

        o_rows, x_rows, w8_rows, w4_codes = {}, {}, {}, {}

        def load_o(pair):
            for half in HALVES:
                t = keep.tile([P, 8 * 2 * DH], BF16, name="o_rows%d_%d" % (pair, half), align_bytes=64)
                rows = o[8 * half : 8 * half + 8, pair * 2 * P : (pair + 1) * 2 * P, :].rearrange("h (p j) d -> p h (j d)", j=2)
                nc.sync.dma_start(out=t[:].rearrange("p (h e) -> p h e", h=8), in_=rows)
                o_rows[pair, half] = t

        def load_x(pair, first, last):
            t = keep.tile([P, 2, (last - first) * CHUNK], BF16, name="x_rows%d_%d" % (pair, first))
            rows = x[pair * 2 * P : (pair + 1) * 2 * P, first * CHUNK : last * CHUNK]
            nc.sync.dma_start(out=t[:], in_=rows.rearrange("(p j) n -> p j n", j=2))
            for chunk in range(first, last):
                x_rows[pair, chunk] = t[:, :, (chunk - first) * CHUNK : (chunk - first + 1) * CHUNK]

        def load_weights(chunk):
            rows = keep.tile([P, PACK, CHUNK], BF16, name="w8_rows%d" % chunk)
            nc.sync.dma_start(out=rows[:], in_=w8[:, chunk * CHUNK : (chunk + 1) * CHUNK].rearrange("(p t) n -> p t n", t=PACK))
            w8_rows[chunk] = rows
            codes = keep.tile([P, W4_PASSES, 2 * CHUNK], U8, name="w4_codes%d" % chunk, align_bytes=64)
            source = w4_words[:, :, 2 * chunk * CHUNK : 2 * (chunk + 1) * CHUNK].rearrange("g p b -> p g b")
            nc.sync.dma_start(out=codes[:].bitcast(I32), in_=source.bitcast(I32))
            w4_codes[chunk] = codes

        def load_w4_scales(scales, first, last):
            for r in range(4):
                rows = w4_scales[:, r:16:4, first:last].rearrange("g q n -> q g n")
                nc.sync.dma_start(out=scales[r:P:32, :, :].bitcast(I32), in_=rows.bitcast(I32))

        bias_rows = keep.tile([P, D // P], BF16, name="bias_rows")
        nc.sync.dma_start(out=bias_rows[:], in_=bias.rearrange("(p c) -> p c", p=P))
        load_o(0)
        load_weights(0)
        load_w4_scales(w4_scales_first, 0, CHUNK)
        load_o(1)
        load_x(0, 0, 1)
        load_x(1, 0, 1)
        load_weights(1)
        load_w4_scales(w4_scales_rest, CHUNK, D)
        load_x(0, 1, CHUNKS)
        load_x(1, 1, CHUNKS)
        load_weights(2)
        load_o(2)
        load_weights(3)

        turn_banks = []

        def next_turn_bank():
            bank = psum.tile([P, 4, P], F32, name="turn%d" % (len(turn_banks) % BANKS))
            turn_banks.append(bank)
            return bank

        bias_all = keep.tile([P, D], BF16, name="bias_all")

        def spread_bias():
            words = bias_rows[:].bitcast(F32)
            spread = bias_all[:].bitcast(F32).rearrange("p (q w) -> p q w", w=8)
            banks = []
            for b in range(2):
                bank = next_turn_bank()
                for n in range(4):
                    w = 4 * b + n
                    nc.tensor.transpose(bank[:, n, :], words[:, w : w + 1].to_broadcast([P, P]), identity[:])
                banks.append(bank)
            for b in range(2):
                nc.scalar.copy(out=spread[:, :, 4 * b : 4 * b + 4], in_=banks[b][:].rearrange("p w q -> p q w"))

        o_sorted, a_banks, a_grouped, a_codes, a_scales = {}, {}, {}, {}, {}

        def sort_o(tile, copy):
            for half in HALVES:
                t = flow.tile([P, 4 * P], F32, name="o_sorted", bufs=6)
                words = o_rows[tile // 2, half][:].bitcast(F32).rearrange("p (h j w) -> p h j w", h=8, j=2)[:, :, tile % 2, :]
                copy(out=t[:].rearrange("p (g u h w) -> p g u h w", g=2, u=2, h=4), in_=words.rearrange("p (g h) (w u) -> p g u h w", g=2, u=2))
                o_sorted[tile, half] = t

        def turn_o(tile):
            for half in HALVES:
                bank = next_turn_bank()
                for n in range(4):
                    nc.tensor.transpose(bank[:, n, :], o_sorted[tile, half][:, n * P : (n + 1) * P], identity[:])
                a_banks[tile, half] = bank

        def group_a(tile):
            t = flow.tile([P, PASSES * P * PACK], BF16, name="a_grouped", bufs=3, align_bytes=64)
            words = t[:].bitcast(F32).rearrange("p (g r u) -> p g r u", g=PASSES, u=2)
            for half in HALVES:
                nc.scalar.copy(out=words[:, 2 * half : 2 * half + 2, :, :], in_=a_banks[tile, half][:].rearrange("p (g u) r -> p g r u", u=2))
            a_grouped[tile] = t

        def quantise_a(tile):
            codes = keep.tile([P, PASSES * P], U32, name="a_codes%d" % tile, align_bytes=64)
            scales = keep.tile([P, PASSES * P], U8, name="a_scales%d" % tile, align_bytes=64)
            nc.vector.quantize_mx(out=codes[:].bitcast(FP8X4), scales=scales[:], in_=a_grouped[tile][:])
            a_codes[tile], a_scales[tile] = codes, scales

        w8_grouped, w8_codes, w8_scales = {}, {}, {}

        def group_w8(chunk):
            t = flow.tile([P, CHUNK, PACK], BF16, name="w8_grouped", bufs=2, align_bytes=64)
            for copy, first, last in ((nc.vector.tensor_copy, 0, W8_SPLIT), (nc.scalar.copy, W8_SPLIT, CHUNK)):
                copy(out=t[:, first:last, :].rearrange("p (n i) t -> p n t i", i=4),
                     in_=w8_rows[chunk][:, :, first:last].rearrange("p t (n i) -> p n t i", i=4))
            w8_grouped[chunk] = t

        def quantise_w8(chunk):
            codes = keep.tile([P, CHUNK], U32, name="w8_codes%d" % chunk, align_bytes=64)
            scales = keep.tile([P, CHUNK], U8, name="w8_scales%d" % chunk, align_bytes=64)
            nc.vector.quantize_mx(out=codes[:].bitcast(FP8X4), scales=scales[:], in_=w8_grouped[chunk][:].rearrange("p n t -> p (n t)"))
            w8_codes[chunk], w8_scales[chunk] = codes, scales

        addends, products, y_twins = {}, {}, {}

        def add_bias(s):
            chunk, tile = place(s)
            t = flow.tile([P, CHUNK], F32, name="addend", bufs=ADDEND_LEAD + 1)
            nc.vector.tensor_tensor(out=t[:], in0=x_rows[tile // 2, chunk][:, tile % 2, :], in1=bias_all[:, chunk * CHUNK : (chunk + 1) * CHUNK], op=ADD)
            addends[s] = t

        def multiply(s):
            chunk, tile = place(s)
            bank = psum.tile([P, CHUNK], F32, name="product%d" % (s % BANKS))
            for g in PASS_ORDER:
                if g == 0:
                    rhs, rhs_scale = w8_codes[chunk][:].bitcast(FP8X4), w8_scales[chunk][:]
                elif chunk == 0:
                    rhs, rhs_scale = w4_codes[chunk][:, g - 1, :].bitcast(FP4X4), w4_scales_first[:, g - 1, :]
                else:
                    rhs, rhs_scale = w4_codes[chunk][:, g - 1, :].bitcast(FP4X4), w4_scales_rest[:, g - 1, (chunk - 1) * CHUNK : chunk * CHUNK]
                tokens = slice(g * P, (g + 1) * P)
                nc.tensor.matmul_mx(out=bank[:], lhsT=a_codes[tile][:, tokens].bitcast(FP8X4), lhsT_scale=a_scales[tile][:, tokens],
                                    rhs=rhs, rhs_scale=rhs_scale, start=(g == PASS_ORDER[0]), stop=(g == PASS_ORDER[-1]))
            products[s] = bank

        def finish_y(s):
            chunk, tile = place(s)
            j = s % 2
            if j == 0:
                t = flow.tile([P, 2, CHUNK], F32, name="y_twin", bufs=8)
                y_twins[s] = t
            y = y_twins[s - j]
            nc.vector.tensor_tensor(out=y[:, j, :], in0=products[s][:], in1=addends[s][:], op=ADD)
            rows = out_0[(tile - j) * P : (tile - j + 2) * P, chunk * CHUNK : (chunk + 1) * CHUNK].rearrange("(p j) n -> p j n", j=2)
            if s >= STEPS - 2:
                nc.sync.dma_start(out=rows[:, j, :], in_=y[:, j, :])
            elif j == 1:
                nc.sync.dma_start(out=rows, in_=y[:])

        y_sorted, y_banks, y_grouped = {}, {}, {}
        y_scales = keep.tile([P, T], U8, name="y_scales", align_bytes=64)

        def round_y(s):
            t = flow.tile([P, CHUNK], BF16, name="y_sorted", bufs=8, align_bytes=64)
            copy = nc.vector.tensor_copy if s == STEPS - 1 else nc.scalar.copy
            copy(out=t[:].rearrange("p (u q e) -> p u q e", u=2, e=2),
                 in_=y_twins[s - s % 2][:, s % 2, :].rearrange("p (q u e) -> p u q e", u=2, e=2))
            y_sorted[s] = t

        def turn_y(twin):
            bank = next_turn_bank()
            for n in range(4):
                j, u = divmod(n, 2)
                nc.tensor.transpose(bank[:, n, :], y_sorted[twin + j][:].bitcast(F32)[:, u * P : (u + 1) * P], identity[:])
            y_banks[twin] = bank

        def group_y(twin):
            t = flow.tile([P, 2 * P * PACK], BF16, name="y_grouped", bufs=4, align_bytes=64)
            nc.scalar.copy(out=t[:].bitcast(F32).rearrange("p (r j u) -> p r j u", j=2, u=2),
                           in_=y_banks[twin][:].rearrange("p (j u) r -> p r j u", u=2))
            y_grouped[twin] = t

        def quantise_y(twin):
            chunk, tile = place(twin)
            codes = flow.tile([P, 2 * P], U32, name="y_codes", bufs=8, align_bytes=64)
            tokens = slice(P * tile, P * (tile + 2))
            nc.vector.quantize_mx(out=codes[:].bitcast(FP8X4), scales=y_scales[4 * chunk : P, tokens], in_=y_grouped[twin][:])
            nc.sync.dma_start(out=out_1[chunk].rearrange("p m t -> p (m t)").bitcast(I32)[:, tokens], in_=codes[:].bitcast(I32))

        spread_bias()
        sort_o(0, nc.vector.tensor_copy)
        turn_o(0)
        group_a(0)
        sort_o(1, nc.vector.tensor_copy)
        turn_o(1)
        group_w8(0)
        quantise_a(0)
        group_a(1)
        quantise_w8(0)
        quantise_a(1)
        sort_o(2, nc.vector.tensor_copy)
        add_bias(0)
        sort_o(3, nc.scalar.copy)
        add_bias(1)

        for s in range(STEPS + 2):
            early = [s + 2] if s + 2 < EARLY_TILES else []
            if s < STEPS:
                multiply(s)
            for tile in early + late_tile_turned_after(s):
                turn_o(tile)
            for twin in twins_turned_after(s):
                turn_y(twin)
            if s < STEPS:
                finish_y(s)
            for tile in early + late_tile_turned_after(s):
                group_a(tile)
            for twin in twins_turned_after(s):
                group_y(twin)
            if s < STEPS:
                round_y(s)
            for tile in early + late_tile_turned_after(s - QUANTISE_LAG):
                quantise_a(tile)
            for twin in twins_turned_after(s - 1):
                quantise_y(twin)
            if s + ADDEND_LEAD < STEPS:
                add_bias(s + ADDEND_LEAD)
            for tile in late_tile_turned_after(s + SORT_LEAD):
                sort_o(tile, nc.scalar.copy)
            if s < (CHUNKS - 1) * EARLY_TILES:
                if s % EARLY_TILES == 0:
                    group_w8(s // EARLY_TILES + 1)
                if s % EARLY_TILES == 2:
                    quantise_w8(s // EARLY_TILES + 1)
            if late_tile_turned_after(s + LOAD_LEAD + SORT_LEAD) == [TILES - 2]:
                load_o(TILES // 2 - 1)
            for pair in range(EARLY_TILES // 2, TILES // 2):
                if s + LOAD_LEAD + ADDEND_LEAD == pair * 2 * CHUNKS:
                    load_x(pair, 0, CHUNKS)

        for q in range(4):
            nc.scalar.dma_start(out=out_2[:, 4 * q : 4 * q + 4, :].bitcast(I32), in_=y_scales[32 * q : 32 * q + 16, :].bitcast(I32))
